import numpy as np
import ml_dtypes


def mxq(x, axis, fmt="e4m3"):
    dtype, down = {"e4m3": (ml_dtypes.float8_e4m3fn, 7), "e5m2": (ml_dtypes.float8_e5m2, 14)}[fmt]
    v = np.moveaxis(np.asarray(x, np.float32).astype(ml_dtypes.bfloat16).astype(np.float64), axis, -1)
    blocks = v.reshape(v.shape[:-1] + (-1, 32))
    amax = np.abs(blocks).max(-1, keepdims=True)
    byte = np.maximum(np.where(amax > 0, np.frexp(amax)[1] - 1 + 127, 0) - down, 1)
    scale = np.exp2(byte - 127.0)
    codes = (blocks / scale).astype(np.float32).astype(dtype).astype(np.float64)
    return np.moveaxis((codes * scale).reshape(v.shape), -1, axis)


WIDE = False


def mx_kscale(k):
    if not WIDE:
        return np.ones(k)
    levels = np.array([10, -10, 5, -5, 0])
    if k % 512:
        return np.exp2(np.random.permutation(np.resize(levels, k // 32))).repeat(32)
    a = np.empty((k // 512, 16))
    for p in range(k // 512):
        a[p, :8] = np.random.permutation(np.resize(levels, 8))
        for g in range(8):
            far = levels[np.abs(levels - a[p, g]) >= 10]
            a[p, g + 8] = far[np.random.randint(len(far))]
    return np.exp2(a.ravel()).repeat(32)


def f64(x):
    return np.asarray(x).astype(np.float64)


def striped(idx):
    return np.tile(idx.reshape(-1, 16).T, (8, 1)).astype(np.uint16)


def unstriped(offs):
    return offs[:16].T.reshape(-1).astype(np.int64)


def pack_weight(w):
    k, n = w.shape
    w = f64(np.asarray(w, np.float32).astype(ml_dtypes.bfloat16)).reshape(k // 32, 32, n)
    amax = np.abs(w).max(1)
    byte = np.clip(np.where(amax > 0, np.frexp(amax)[1] - 1 + 127 - 7, 1), 1, 254)
    scaled = (w * np.exp2(127.0 - byte)[:, None, :]).reshape(k, n).astype(np.float32)
    words = np.ascontiguousarray(scaled.reshape(k // 512, 128, 4, n).transpose(0, 1, 3, 2)).astype(ml_dtypes.float8_e4m3fn).view(np.uint8)
    return words, np.ascontiguousarray(byte.astype(np.uint8).reshape(k // 512, 16, n))


def unpack_weight(words, scales):
    g, p, n, _ = words.shape
    vals = np.ascontiguousarray(words).view(ml_dtypes.float8_e4m3fn).astype(np.float64) * np.repeat(np.exp2(scales.astype(np.float64) - 127.0), 8, axis=1)[..., None]
    return vals.transpose(0, 1, 3, 2).reshape(g * 512, n)


def relu(v):
    return np.maximum(v, 0.0)


K, T, S, N, H, W = 512, 1024, 512, 256, 512, 2048


def setup_inputs():
    n = np.random.standard_normal
    s = mx_kscale(K)[:, None]
    u = mx_kscale(H)
    packed_xT = pack_weight(n((K, T)) * s)
    packed_eT = pack_weight(n((K, W)) * s)
    return {
        "x_words": packed_xT[0],
        "x_scales": packed_xT[1],
        "w1": (n((K, H)) / np.sqrt(K) / s).astype(np.float32),
        "e_words": packed_eT[0],
        "e_scales": packed_eT[1],
        "w2": (n((K, H)) / np.sqrt(K) / s).astype(np.float32),
        "thr": (-np.random.uniform(0.2, 0.8, (H, 1))).astype(np.float32),
        "unit": (np.random.uniform(0.6, 1.4, (H, 1)) * u[:, None]).astype(np.float32),
        "w3": (n((H, N)) / np.sqrt(H) / u[:, None]).astype(np.float32),
        "tgt": (n((N, S))).astype(np.float32),
        "offs": striped(np.random.permutation(T)[:S]),
        "mate": striped(np.random.permutation(W)[:S]),
        "fold": striped(np.random.permutation(S)),
    }


def reference(x_words, x_scales, w1, e_words, e_scales, w2, thr, unit, w3, tgt, offs, mate, fold):
    xq = unpack_weight(x_words, x_scales)[:, unstriped(offs)]
    y = mxq(f64(w1), 0, "e4m3").T @ xq
    e_mate = unpack_weight(e_words, e_scales)[:, unstriped(mate)]
    ye = mxq(f64(w2), 0, "e4m3").T @ e_mate
    lat = relu(y + ye + f64(thr))
    ff = lat[:, unstriped(fold)]
    mx = np.maximum(lat, 0.8 * ff)
    hid = f64(unit) * (mx * (y - ye))
    rr = mxq(f64(w3), 0, "e4m3").T @ mxq(hid, 0, "e4m3")
    return f64(tgt) - rr

@@ -1,0 +1,206 @@
+from contextlib import ExitStack
+
+import concourse.mybir as mybir
+
+K, T, S, N, H, W = 512, 1024, 512, 256, 512, 2048
+FLOPS = 2 * (2 * K * H * S + H * N * S)
+
+F32 = mybir.dt.float32
+BF16 = mybir.dt.bfloat16
+I32 = mybir.dt.int32
+U32 = mybir.dt.uint32
+U16 = mybir.dt.uint16
+U8 = mybir.dt.uint8
+FP8X4 = mybir.dt.float8_e4m3fn_x4
+ALU = mybir.AluOpType
+ACT = mybir.ActivationFunctionType
+
+P = 128
+PACK = 4
+SUMMED = 2
+CHUNK = 128
+
+
+def tile_picked_ysaecr_dif_p_kernel(
+    tc, x_words, x_scales, w1, e_words, e_scales, w2, thr, unit, w3, tgt, offs, mate, fold, out
+):
+    nc = tc.nc
+    with ExitStack() as ctx:
+        keep = ctx.enter_context(tc.tile_pool(name="keep", bufs=1))
+        psum = ctx.enter_context(tc.psum_pool(name="psum", bufs=1))
+
+        def sb(name, shape, dtype):
+            return keep.tile(shape, dtype, name=name, align_bytes=64)
+
+        offs_sb = sb("offs_sb", [P, S // 16], U16)
+        mate_sb = sb("mate_sb", [P, S // 16], U16)
+        fold_sb = sb("fold_sb", [P, S // 16], U16)
+        xw = sb("xw", [P, T], U32)
+        xs = sb("xs", [P, T], U8)
+        ew = sb("ew", [P, W], U32)
+        es = sb("es", [P, W], U8)
+        half = H // 2
+        w1_raw = [sb("w1_raw%d" % h, [P, PACK, half], F32) for h in range(2)]
+        w2_raw = [sb("w2_raw%d" % h, [P, PACK, half], F32) for h in range(2)]
+        w3_raw = sb("w3_raw", [P, PACK, N], F32)
+        tgt_sb = sb("tgt_sb", [P, N // P, S], F32)
+        thr_sb = sb("thr_sb", [P, PACK], F32)
+        unit_sb = sb("unit_sb", [P, PACK], F32)
+
+        def load_scales(queue, plane, scales):
+            for q in range(4):
+                queue.dma_start(
+                    out=plane[32 * q : 32 * q + 4, :].bitcast(I32),
+                    in_=scales[0, 4 * q : 4 * q + 4, :].bitcast(I32),
+                )
+
+        def load_weight(raw, w):
+            rows = w.rearrange("(p j) c -> p j c", j=PACK)
+            for h in range(2):
+                nc.sync.dma_start(out=raw[h][:], in_=rows[:, :, h * half : (h + 1) * half])
+
+        nc.vector.memset(xs[:].bitcast(I32), 0)
+        nc.vector.memset(es[:].bitcast(I32), 0)
+        nc.sync.dma_start(offs_sb[:], offs)
+        nc.sync.dma_start(out=xw[:].bitcast(I32), in_=x_words[0].rearrange("p n t -> p (n t)").bitcast(I32))
+        load_scales(nc.scalar, xs, x_scales)
+        load_weight(w1_raw, w1)
+        nc.sync.dma_start(mate_sb[:], mate)
+        load_scales(nc.scalar, es, e_scales)
+        load_weight(w2_raw, w2)
+        nc.sync.dma_start(out=ew[:].bitcast(I32), in_=e_words[0].rearrange("p n t -> p (n t)").bitcast(I32))
+        nc.sync.dma_start(fold_sb[:], fold)
+        nc.gpsimd.dma_start(out=thr_sb[:], in_=thr.rearrange("(p t) o -> p (t o)", t=PACK))
+        nc.gpsimd.dma_start(out=unit_sb[:], in_=unit.rearrange("(p t) o -> p (t o)", t=PACK))
+        nc.sync.dma_start(out=w3_raw[:], in_=w3.rearrange("(p j) n -> p j n", j=PACK))
+        nc.sync.dma_start(out=tgt_sb[:], in_=tgt.rearrange("(a p) s -> p a s", p=P))
+
+        unit_neg = sb("unit_neg", [P, PACK], F32)
+        unit_two = sb("unit_two", [P, PACK], F32)
+        nc.gpsimd.tensor_scalar(unit_neg[:], unit_sb[:], -1.0, 0.0, ALU.mult, ALU.add)
+        nc.gpsimd.tensor_scalar(unit_two[:], unit_sb[:], 2.0, 0.0, ALU.mult, ALU.add)
+
+        xw_g = sb("xw_g", [P, S], U32)
+        xs_g = sb("xs_g", [P, S], U8)
+        ew_g = sb("ew_g", [P, S], U32)
+        es_g = sb("es_g", [P, S], U8)
+
+        def deal(copy, grouped, raw, h):
+            dst = grouped[:, :, h * (P // 2) : (h + 1) * (P // 2), :].rearrange("p t m j -> p m j t")
+            copy(out=dst, in_=raw[h][:].rearrange("p j (m t) -> p m j t", t=PACK))
+
+        w1_bf = sb("w1_bf", [P, PACK, P, PACK], BF16)
+        w2_bf = sb("w2_bf", [P, PACK, P, PACK], BF16)
+        w1_q = sb("w1_q", [P, H], U32)
+        w1_s = sb("w1_s", [P, H], U8)
+        w2_q = sb("w2_q", [P, H], U32)
+        w2_s = sb("w2_s", [P, H], U8)
+
+        nc.vector.tensor_copy(out=xs_g[:], in_=xs[:].indirect(offs_sb[:]))
+        nc.vector.tensor_copy(out=xw_g[:], in_=xw[:].indirect(offs_sb[:]))
+        deal(nc.scalar.copy, w1_bf, w1_raw, 0)
+        deal(nc.vector.tensor_copy, w1_bf, w1_raw, 1)
+        nc.vector.tensor_copy(out=es_g[:], in_=es[:].indirect(mate_sb[:]))
+        nc.vector.quantize_mx(out=w1_q[:].bitcast(FP8X4), scales=w1_s[:], in_=w1_bf[:].rearrange("p t m j -> p (t m j)"))
+        deal(nc.scalar.copy, w2_bf, w2_raw, 0)
+        deal(nc.scalar.copy, w2_bf, w2_raw, 1)
+        nc.vector.quantize_mx(out=w2_q[:].bitcast(FP8X4), scales=w2_s[:], in_=w2_bf[:].rearrange("p t m j -> p (t m j)"))
+
+        def encode(bank, wq, ws, words, scales, t, start, stop):
+            cols = slice(t * P, (t + 1) * P)
+            nc.tensor.matmul_mx(
+                out=bank[:], lhsT=wq[:, cols].bitcast(FP8X4), lhsT_scale=ws[:, cols],
+                rhs=words[:].bitcast(FP8X4), rhs_scale=scales[:], start=start, stop=stop,
+            )
+
+        y_bank = [psum.tile([P, S], F32, name="y_bank%d" % t, tag="bank%d" % t) for t in range(PACK)]
+        e_bank = [psum.tile([P, S], F32, name="e_bank%d" % t, tag="bank%d" % (PACK + t)) for t in range(PACK)]
+        lat = [sb("lat%d" % t, [P, 2 * S], F32) for t in range(PACK)]
+        y_sb = [sb("y_sb%d" % t, [P, S], F32) for t in range(SUMMED, PACK)]
+        for t in range(PACK):
+            encode(y_bank[t], w1_q, w1_s, xw_g, xs_g, t, True, True)
+        for t in range(SUMMED):
+            encode(e_bank[t], w1_q, w1_s, xw_g, xs_g, t, True, False)
+        for t in range(SUMMED):
+            nc.scalar.activation(lat[t][:, S:], y_bank[t][:], ACT.Copy, scale=unit_two[:, t : t + 1])
+        for t in range(SUMMED, PACK):
+            nc.scalar.copy(out=y_sb[t - SUMMED][:], in_=y_bank[t][:])
+
+        nc.vector.tensor_copy(out=ew_g[:], in_=ew[:].indirect(mate_sb[:]))
+        for t in range(PACK):
+            encode(e_bank[t], w2_q, w2_s, ew_g, es_g, t, t >= SUMMED, True)
+
+        diff = sb("diff", [P, PACK, S], F32)
+        best = sb("best", [P, PACK, S], F32)
+        ff = [sb("ff%d" % t, [P, S], F32) for t in range(PACK)]
+        pre = [sb("pre%d" % t, [P, S], F32) for t in range(SUMMED, PACK)]
+
+        def scaled_diff(t):
+            nc.vector.scalar_tensor_tensor(diff[:, t, :], e_bank[t][:], unit_neg[:, t : t + 1], lat[t][:, S:], ALU.mult, ALU.add)
+
+        def fetch(t):
+            nc.vector.tensor_copy(out=ff[t][:], in_=lat[t][:].indirect(fold_sb[:]))
+
+        def compete(t):
+            nc.vector.scalar_tensor_tensor(best[:, t, :], ff[t][:], 0.8, lat[t][:, :S], ALU.mult, ALU.max)
+
+        for t in range(SUMMED):
+            nc.scalar.activation(lat[t][:, :S], e_bank[t][:], ACT.Relu, bias=thr_sb[:, t : t + 1])
+        scaled_diff(0)
+        fetch(0)
+        for t in range(SUMMED, PACK):
+            nc.vector.scalar_tensor_tensor(pre[t - SUMMED][:], e_bank[t][:], thr_sb[:, t : t + 1], y_sb[t - SUMMED][:], ALU.add, ALU.add)
+            nc.scalar.activation(lat[t][:, S:], y_bank[t][:], ACT.Copy, scale=unit_sb[:, t : t + 1])
+            nc.scalar.activation(lat[t][:, :S], pre[t - SUMMED][:], ACT.Relu)
+        w3_bf = sb("w3_bf", [P, N, PACK], BF16)
+        w3_q = sb("w3_q", [P, N], U32)
+        w3_s = sb("w3_s", [P, N], U8)
+        nc.scalar.copy(
+            out=w3_bf[:].rearrange("p (c i) j -> p c j i", i=4),
+            in_=w3_raw[:].rearrange("p j (c i) -> p c j i", i=4),
+        )
+        for t in range(1, PACK):
+            fetch(t)
+            compete(t - 1)
+            scaled_diff(t)
+        compete(PACK - 1)
+        nc.vector.quantize_mx(out=w3_q[:].bitcast(FP8X4), scales=w3_s[:], in_=w3_bf[:].rearrange("p n j -> p (n j)"))
+
+        chunks = S // CHUNK
+        hid = [sb("hid%d" % c, [P, CHUNK, PACK], BF16) for c in range(chunks)]
+        hid_q = [sb("hid_q%d" % c, [P, CHUNK], U32) for c in range(chunks)]
+        hid_s = [sb("hid_s%d" % c, [P, CHUNK], U8) for c in range(chunks)]
+        res = [sb("res%d" % c, [P, N // P, CHUNK], F32) for c in range(chunks)]
+        r_bank = [psum.tile([P, N // P, CHUNK], F32, name="r_bank%d" % c, tag="bank%d" % c) for c in range(chunks)]
+        out_rows = out.rearrange("(a p) s -> p a s", p=P)
+
+        def product(c):
+            cols = slice(c * CHUNK, (c + 1) * CHUNK)
+            nc.vector.tensor_tensor(
+                hid[c][:].rearrange("p (g i) t -> p g t i", i=4),
+                best[:, :, cols].rearrange("p t (g i) -> p g t i", i=4),
+                diff[:, :, cols].rearrange("p t (g i) -> p g t i", i=4),
+                ALU.mult,
+            )
+
+        def decode(c):
+            nc.vector.quantize_mx(out=hid_q[c][:].bitcast(FP8X4), scales=hid_s[c][:], in_=hid[c][:].rearrange("p s t -> p (s t)"))
+            for a in range(N // P):
+                rows = slice(a * P, (a + 1) * P)
+                nc.tensor.matmul_mx(
+                    out=r_bank[c][:, a, :], lhsT=w3_q[:, rows].bitcast(FP8X4), lhsT_scale=w3_s[:, rows],
+                    rhs=hid_q[c][:].bitcast(FP8X4), rhs_scale=hid_s[c][:], start=True, stop=True,
+                )
+
+        def finish(c):
+            cols = slice(c * CHUNK, (c + 1) * CHUNK)
+            nc.vector.tensor_tensor(res[c][:], tgt_sb[:, :, cols], r_bank[c][:], ALU.subtract)
+            nc.sync.dma_start(out=out_rows[:, :, cols], in_=res[c][:])
+
+        for step in range(chunks + 2):
+            if step < chunks:
+                product(step)
+            if 1 <= step <= chunks:
+                decode(step - 1)
+            if step >= 2:
+                finish(step - 2)

@@ -29,8 +29,8 @@ def tile_picked_ysaecr_dif_p_kernel(
         keep = ctx.enter_context(tc.tile_pool(name="keep", bufs=1))
         psum = ctx.enter_context(tc.psum_pool(name="psum", bufs=1))
 
-        def sb(name, shape, dtype):
-            return keep.tile(shape, dtype, name=name, align_bytes=64)
+        def sb(name, shape, dtype, tag=None):
+            return keep.tile(shape, dtype, name=name, tag=tag or name, align_bytes=64)
 
         offs_sb = sb("offs_sb", [P, S // 16], U16)
         mate_sb = sb("mate_sb", [P, S // 16], U16)
@@ -40,10 +40,8 @@ def tile_picked_ysaecr_dif_p_kernel(
         ew = sb("ew", [P, W], U32)
         es = sb("es", [P, W], U8)
         half = H // 2
-        w1_raw = [sb("w1_raw%d" % h, [P, PACK, half], F32) for h in range(2)]
-        w2_raw = [sb("w2_raw%d" % h, [P, PACK, half], F32) for h in range(2)]
-        w3_raw = sb("w3_raw", [P, PACK, N], F32)
-        tgt_sb = sb("tgt_sb", [P, N // P, S], F32)
+        w1_raw = sb("w1_raw", [P, PACK, H], F32)
+        w2_raw = sb("w2_raw", [P, PACK, H], F32)
         thr_sb = sb("thr_sb", [P, PACK], F32)
         unit_sb = sb("unit_sb", [P, PACK], F32)
 
@@ -55,39 +53,44 @@ def tile_picked_ysaecr_dif_p_kernel(
                 )
 
         def load_weight(raw, w):
-            rows = w.rearrange("(p j) c -> p j c", j=PACK)
-            for h in range(2):
-                nc.sync.dma_start(out=raw[h][:], in_=rows[:, :, h * half : (h + 1) * half])
+            nc.sync.dma_start(out=raw[:], in_=w.rearrange("(p j) c -> p j c", j=PACK))
 
         nc.vector.memset(xs[:].bitcast(I32), 0)
-        nc.vector.memset(es[:].bitcast(I32), 0)
+        nc.gpsimd.memset(es[:].bitcast(I32), 0)
         nc.sync.dma_start(offs_sb[:], offs)
+        nc.sync.dma_start(mate_sb[:], mate)
+        nc.sync.dma_start(fold_sb[:], fold)
         nc.sync.dma_start(out=xw[:].bitcast(I32), in_=x_words[0].rearrange("p n t -> p (n t)").bitcast(I32))
         load_scales(nc.scalar, xs, x_scales)
         load_weight(w1_raw, w1)
-        nc.sync.dma_start(mate_sb[:], mate)
-        load_scales(nc.scalar, es, e_scales)
         load_weight(w2_raw, w2)
         nc.sync.dma_start(out=ew[:].bitcast(I32), in_=e_words[0].rearrange("p n t -> p (n t)").bitcast(I32))
-        nc.sync.dma_start(fold_sb[:], fold)
-        nc.gpsimd.dma_start(out=thr_sb[:], in_=thr.rearrange("(p t) o -> p (t o)", t=PACK))
-        nc.gpsimd.dma_start(out=unit_sb[:], in_=unit.rearrange("(p t) o -> p (t o)", t=PACK))
-        nc.sync.dma_start(out=w3_raw[:], in_=w3.rearrange("(p j) n -> p j n", j=PACK))
-        nc.sync.dma_start(out=tgt_sb[:], in_=tgt.rearrange("(a p) s -> p a s", p=P))
+        load_scales(nc.gpsimd, es, e_scales)
+        nc.scalar.dma_start(out=unit_sb[:], in_=unit.rearrange("(p t) o -> p (t o)", t=PACK))
+        nc.scalar.dma_start(out=thr_sb[:], in_=thr.rearrange("(p t) o -> p (t o)", t=PACK))
 
         unit_neg = sb("unit_neg", [P, PACK], F32)
         unit_two = sb("unit_two", [P, PACK], F32)
         nc.gpsimd.tensor_scalar(unit_neg[:], unit_sb[:], -1.0, 0.0, ALU.mult, ALU.add)
         nc.gpsimd.tensor_scalar(unit_two[:], unit_sb[:], 2.0, 0.0, ALU.mult, ALU.add)
 
+        thr_part = sb("thr_part", [P, PACK], F32)
+        nc.gpsimd.tensor_scalar(thr_part[:], thr_sb[:], 0.8, 0.0, ALU.mult, ALU.add)
+
         xw_g = sb("xw_g", [P, S], U32)
         xs_g = sb("xs_g", [P, S], U8)
-        ew_g = sb("ew_g", [P, S], U32)
-        es_g = sb("es_g", [P, S], U8)
 
         def deal(copy, grouped, raw, h):
-            dst = grouped[:, :, h * (P // 2) : (h + 1) * (P // 2), :].rearrange("p t m j -> p m j t")
-            copy(out=dst, in_=raw[h][:].rearrange("p j (m t) -> p m j t", t=PACK))
+            pair = slice(2 * h, 2 * h + 2)
+            dst = grouped[:, pair, :, :].rearrange("p t m j -> p m j t")
+            copy(out=dst, in_=raw[:].rearrange("p j (m t) -> p m j t", t=PACK)[:, :, :, pair])
+
+        def quantize(codes, scales, grouped, h):
+            cols = slice(h * half, (h + 1) * half)
+            nc.vector.quantize_mx(
+                out=codes[:, cols].bitcast(FP8X4), scales=scales[:, cols],
+                in_=grouped[:, 2 * h : 2 * h + 2, :, :].rearrange("p t m j -> p (t m j)"),
+            )
 
         w1_bf = sb("w1_bf", [P, PACK, P, PACK], BF16)
         w2_bf = sb("w2_bf", [P, PACK, P, PACK], BF16)
@@ -96,15 +99,22 @@ def tile_picked_ysaecr_dif_p_kernel(
         w2_q = sb("w2_q", [P, H], U32)
         w2_s = sb("w2_s", [P, H], U8)
 
-        nc.vector.tensor_copy(out=xs_g[:], in_=xs[:].indirect(offs_sb[:]))
         nc.vector.tensor_copy(out=xw_g[:], in_=xw[:].indirect(offs_sb[:]))
+        nc.vector.tensor_copy(out=xs_g[:], in_=xs[:].indirect(offs_sb[:]))
         deal(nc.scalar.copy, w1_bf, w1_raw, 0)
         deal(nc.vector.tensor_copy, w1_bf, w1_raw, 1)
+        w3_raw = sb("w3_raw", [P, PACK, N], F32, tag="w1_raw")
+        nc.sync.dma_start(out=w3_raw[:], in_=w3.rearrange("(p j) n -> p j n", j=PACK))
+        quantize(w1_q, w1_s, w1_bf, 1)
+        quantize(w1_q, w1_s, w1_bf, 0)
+        es_g = sb("es_g", [P, S], U8, tag="w1_bf")
         nc.vector.tensor_copy(out=es_g[:], in_=es[:].indirect(mate_sb[:]))
-        nc.vector.quantize_mx(out=w1_q[:].bitcast(FP8X4), scales=w1_s[:], in_=w1_bf[:].rearrange("p t m j -> p (t m j)"))
         deal(nc.scalar.copy, w2_bf, w2_raw, 0)
-        deal(nc.scalar.copy, w2_bf, w2_raw, 1)
-        nc.vector.quantize_mx(out=w2_q[:].bitcast(FP8X4), scales=w2_s[:], in_=w2_bf[:].rearrange("p t m j -> p (t m j)"))
+        deal(nc.vector.tensor_copy, w2_bf, w2_raw, 1)
+        tgt_sb = sb("tgt_sb", [P, N // P, S], F32, tag="w2_raw")
+        nc.sync.dma_start(out=tgt_sb[:], in_=tgt.rearrange("(a p) s -> p a s", p=P))
+        quantize(w2_q, w2_s, w2_bf, 1)
+        quantize(w2_q, w2_s, w2_bf, 0)
 
         def encode(bank, wq, ws, words, scales, t, start, stop):
             cols = slice(t * P, (t + 1) * P)
@@ -116,24 +126,31 @@ def tile_picked_ysaecr_dif_p_kernel(
         y_bank = [psum.tile([P, S], F32, name="y_bank%d" % t, tag="bank%d" % t) for t in range(PACK)]
         e_bank = [psum.tile([P, S], F32, name="e_bank%d" % t, tag="bank%d" % (PACK + t)) for t in range(PACK)]
         lat = [sb("lat%d" % t, [P, 2 * S], F32) for t in range(PACK)]
-        y_sb = [sb("y_sb%d" % t, [P, S], F32) for t in range(SUMMED, PACK)]
-        for t in range(PACK):
+        for t in reversed(range(PACK)):
             encode(y_bank[t], w1_q, w1_s, xw_g, xs_g, t, True, True)
         for t in range(SUMMED):
             encode(e_bank[t], w1_q, w1_s, xw_g, xs_g, t, True, False)
+        for t in range(SUMMED, PACK):
+            nc.scalar.copy(out=lat[t][:, S:], in_=y_bank[t][:])
         for t in range(SUMMED):
             nc.scalar.activation(lat[t][:, S:], y_bank[t][:], ACT.Copy, scale=unit_two[:, t : t + 1])
-        for t in range(SUMMED, PACK):
-            nc.scalar.copy(out=y_sb[t - SUMMED][:], in_=y_bank[t][:])
 
+        ew_g = sb("ew_g", [P, S], U32, tag="es")
         nc.vector.tensor_copy(out=ew_g[:], in_=ew[:].indirect(mate_sb[:]))
-        for t in range(PACK):
+        for t in (0, 2, 1, 3):
             encode(e_bank[t], w2_q, w2_s, ew_g, es_g, t, t >= SUMMED, True)
 
         diff = sb("diff", [P, PACK, S], F32)
         best = sb("best", [P, PACK, S], F32)
         ff = [sb("ff%d" % t, [P, S], F32) for t in range(PACK)]
-        pre = [sb("pre%d" % t, [P, S], F32) for t in range(SUMMED, PACK)]
+        ye_sb = {t: sb("ye_sb%d" % t, [P, S], F32) for t in range(SUMMED, PACK)}
+        total = {t: sb("total%d" % t, [P, S], F32) for t in range(SUMMED, PACK)}
+        plain = {t: sb("plain%d" % t, [P, S], F32) for t in range(SUMMED, PACK)}
+        for t in range(SUMMED):
+            total[t] = e_bank[t]
+
+        def latent(t):
+            nc.scalar.activation(lat[t][:, :S], total[t][:], ACT.Relu, bias=thr_part[:, t : t + 1], scale=0.8)
 
         def scaled_diff(t):
             nc.vector.scalar_tensor_tensor(diff[:, t, :], e_bank[t][:], unit_neg[:, t : t + 1], lat[t][:, S:], ALU.mult, ALU.add)
@@ -142,16 +159,17 @@ def tile_picked_ysaecr_dif_p_kernel(
             nc.vector.tensor_copy(out=ff[t][:], in_=lat[t][:].indirect(fold_sb[:]))
 
         def compete(t):
-            nc.vector.scalar_tensor_tensor(best[:, t, :], ff[t][:], 0.8, lat[t][:, :S], ALU.mult, ALU.max)
+            nc.vector.scalar_tensor_tensor(best[:, t, :], total[t][:], thr_sb[:, t : t + 1], ff[t][:], ALU.add, ALU.max)
 
         for t in range(SUMMED):
-            nc.scalar.activation(lat[t][:, :S], e_bank[t][:], ACT.Relu, bias=thr_sb[:, t : t + 1])
-        scaled_diff(0)
-        fetch(0)
+            latent(t)
+            nc.scalar.copy(out=ye_sb[SUMMED + t][:], in_=e_bank[SUMMED + t][:])
         for t in range(SUMMED, PACK):
-            nc.vector.scalar_tensor_tensor(pre[t - SUMMED][:], e_bank[t][:], thr_sb[:, t : t + 1], y_sb[t - SUMMED][:], ALU.add, ALU.add)
-            nc.scalar.activation(lat[t][:, S:], y_bank[t][:], ACT.Copy, scale=unit_sb[:, t : t + 1])
-            nc.scalar.activation(lat[t][:, :S], pre[t - SUMMED][:], ACT.Relu)
+            nc.gpsimd.tensor_tensor(total[t][:], lat[t][:, S:], ye_sb[t][:], ALU.add)
+            latent(t)
+        for t in range(SUMMED, PACK):
+            nc.gpsimd.tensor_tensor(plain[t][:], lat[t][:, S:], ye_sb[t][:], ALU.subtract)
+            nc.scalar.activation(diff[:, t, :], plain[t][:], ACT.Copy, scale=unit_sb[:, t : t + 1])
         w3_bf = sb("w3_bf", [P, N, PACK], BF16)
         w3_q = sb("w3_q", [P, N], U32)
         w3_s = sb("w3_s", [P, N], U8)
@@ -159,10 +177,12 @@ def tile_picked_ysaecr_dif_p_kernel(
             out=w3_bf[:].rearrange("p (c i) j -> p c j i", i=4),
             in_=w3_raw[:].rearrange("p j (c i) -> p c j i", i=4),
         )
+        scaled_diff(0)
+        fetch(0)
+        scaled_diff(1)
         for t in range(1, PACK):
-            fetch(t)
             compete(t - 1)
-            scaled_diff(t)
+            fetch(t)
         compete(PACK - 1)
         nc.vector.quantize_mx(out=w3_q[:].bitcast(FP8X4), scales=w3_s[:], in_=w3_bf[:].rearrange("p n j -> p (n j)"))
 

@@ -18,7 +18,8 @@ ACT = mybir.ActivationFunctionType
 P = 128
 PACK = 4
 SUMMED = 2
-CHUNK = 128
+CHUNKS = (128, 128, 128, 128)
+WINDOW = 704
 
 
 def tile_picked_ysaecr_dif_p_kernel(
@@ -56,18 +57,18 @@ def tile_picked_ysaecr_dif_p_kernel(
             nc.sync.dma_start(out=raw[:], in_=w.rearrange("(p j) c -> p j c", j=PACK))
 
         nc.vector.memset(xs[:].bitcast(I32), 0)
-        nc.gpsimd.memset(es[:].bitcast(I32), 0)
+        nc.vector.memset(es[:].bitcast(I32), 0)
         nc.sync.dma_start(offs_sb[:], offs)
+        nc.sync.dma_start(out=xw[:].bitcast(I32), in_=x_words[0].rearrange("p n t -> p (n t)").bitcast(I32))
+        load_scales(nc.sync, xs, x_scales)
+        load_weight(w1_raw, w1)
         nc.sync.dma_start(mate_sb[:], mate)
         nc.sync.dma_start(fold_sb[:], fold)
-        nc.sync.dma_start(out=xw[:].bitcast(I32), in_=x_words[0].rearrange("p n t -> p (n t)").bitcast(I32))
-        load_scales(nc.scalar, xs, x_scales)
-        load_weight(w1_raw, w1)
+        load_scales(nc.sync, es, e_scales)
         load_weight(w2_raw, w2)
         nc.sync.dma_start(out=ew[:].bitcast(I32), in_=e_words[0].rearrange("p n t -> p (n t)").bitcast(I32))
-        load_scales(nc.gpsimd, es, e_scales)
-        nc.scalar.dma_start(out=unit_sb[:], in_=unit.rearrange("(p t) o -> p (t o)", t=PACK))
-        nc.scalar.dma_start(out=thr_sb[:], in_=thr.rearrange("(p t) o -> p (t o)", t=PACK))
+        nc.gpsimd.dma_start(out=unit_sb[:], in_=unit.rearrange("(p t) o -> p (t o)", t=PACK))
+        nc.gpsimd.dma_start(out=thr_sb[:], in_=thr.rearrange("(p t) o -> p (t o)", t=PACK))
 
         unit_neg = sb("unit_neg", [P, PACK], F32)
         unit_two = sb("unit_two", [P, PACK], F32)
@@ -111,7 +112,7 @@ def tile_picked_ysaecr_dif_p_kernel(
         nc.vector.tensor_copy(out=es_g[:], in_=es[:].indirect(mate_sb[:]))
         deal(nc.scalar.copy, w2_bf, w2_raw, 0)
         deal(nc.vector.tensor_copy, w2_bf, w2_raw, 1)
-        tgt_sb = sb("tgt_sb", [P, N // P, S], F32, tag="w2_raw")
+        tgt_sb = sb("tgt_sb", [P, N // P, S], F32, tag="xw")
         nc.sync.dma_start(out=tgt_sb[:], in_=tgt.rearrange("(a p) s -> p a s", p=P))
         quantize(w2_q, w2_s, w2_bf, 1)
         quantize(w2_q, w2_s, w2_bf, 0)
@@ -125,18 +126,23 @@ def tile_picked_ysaecr_dif_p_kernel(
 
         y_bank = [psum.tile([P, S], F32, name="y_bank%d" % t, tag="bank%d" % t) for t in range(PACK)]
         e_bank = [psum.tile([P, S], F32, name="e_bank%d" % t, tag="bank%d" % (PACK + t)) for t in range(PACK)]
-        lat = [sb("lat%d" % t, [P, 2 * S], F32) for t in range(PACK)]
+        lat = [sb("lat%d" % t, [P, WINDOW], F32) for t in range(PACK)]
+        for t in range(PACK):
+            nc.gpsimd.memset(lat[t][:, S:], 0.0)
+        y_sb = sb("y_sb", [P, PACK - 1, S], F32, tag="w2_raw")
         for t in reversed(range(PACK)):
             encode(y_bank[t], w1_q, w1_s, xw_g, xs_g, t, True, True)
         for t in range(SUMMED):
             encode(e_bank[t], w1_q, w1_s, xw_g, xs_g, t, True, False)
         for t in range(SUMMED, PACK):
-            nc.scalar.copy(out=lat[t][:, S:], in_=y_bank[t][:])
-        for t in range(SUMMED):
-            nc.scalar.activation(lat[t][:, S:], y_bank[t][:], ACT.Copy, scale=unit_two[:, t : t + 1])
+            nc.scalar.copy(out=y_sb[:, t - SUMMED, :], in_=y_bank[t][:])
+        nc.scalar.activation(y_sb[:, 2, :], y_bank[1][:], ACT.Copy, scale=unit_two[:, 1:2])
 
         ew_g = sb("ew_g", [P, S], U32, tag="es")
         nc.vector.tensor_copy(out=ew_g[:], in_=ew[:].indirect(mate_sb[:]))
+        y_first = sb("y_first", [P, S], F32, tag="ew")
+        nc.vector.tensor_scalar(y_first[:], y_bank[0][:], unit_two[:, 0:1], None, ALU.mult)
+        twice = [y_first[:], y_sb[:, 2, :]]
         for t in (0, 2, 1, 3):
             encode(e_bank[t], w2_q, w2_s, ew_g, es_g, t, t >= SUMMED, True)
 
@@ -153,7 +159,7 @@ def tile_picked_ysaecr_dif_p_kernel(
             nc.scalar.activation(lat[t][:, :S], total[t][:], ACT.Relu, bias=thr_part[:, t : t + 1], scale=0.8)
 
         def scaled_diff(t):
-            nc.vector.scalar_tensor_tensor(diff[:, t, :], e_bank[t][:], unit_neg[:, t : t + 1], lat[t][:, S:], ALU.mult, ALU.add)
+            nc.vector.scalar_tensor_tensor(diff[:, t, :], e_bank[t][:], unit_neg[:, t : t + 1], twice[t], ALU.mult, ALU.add)
 
         def fetch(t):
             nc.vector.tensor_copy(out=ff[t][:], in_=lat[t][:].indirect(fold_sb[:]))
@@ -165,37 +171,41 @@ def tile_picked_ysaecr_dif_p_kernel(
             latent(t)
             nc.scalar.copy(out=ye_sb[SUMMED + t][:], in_=e_bank[SUMMED + t][:])
         for t in range(SUMMED, PACK):
-            nc.gpsimd.tensor_tensor(total[t][:], lat[t][:, S:], ye_sb[t][:], ALU.add)
-            latent(t)
-        for t in range(SUMMED, PACK):
-            nc.gpsimd.tensor_tensor(plain[t][:], lat[t][:, S:], ye_sb[t][:], ALU.subtract)
-            nc.scalar.activation(diff[:, t, :], plain[t][:], ACT.Copy, scale=unit_sb[:, t : t + 1])
-        w3_bf = sb("w3_bf", [P, N, PACK], BF16)
+            nc.gpsimd.tensor_tensor(total[t][:], y_sb[:, t - SUMMED, :], ye_sb[t][:], ALU.add)
+        latent(2)
+        scaled_diff(0)
+        fetch(0)
+        scaled_diff(1)
+        fetch(1)
+        w3_bf = sb("w3_bf", [P, N, PACK], BF16, tag="lat1")
         w3_q = sb("w3_q", [P, N], U32)
         w3_s = sb("w3_s", [P, N], U8)
         nc.scalar.copy(
             out=w3_bf[:].rearrange("p (c i) j -> p c j i", i=4),
             in_=w3_raw[:].rearrange("p j (c i) -> p c j i", i=4),
         )
-        scaled_diff(0)
-        fetch(0)
-        scaled_diff(1)
-        for t in range(1, PACK):
-            compete(t - 1)
+        latent(3)
+        for t in range(SUMMED, PACK):
+            nc.gpsimd.tensor_tensor(plain[t][:], y_sb[:, t - SUMMED, :], ye_sb[t][:], ALU.subtract)
+            nc.scalar.activation(diff[:, t, :], plain[t][:], ACT.Copy, scale=unit_sb[:, t : t + 1])
+        for t in range(SUMMED, PACK):
+            compete(t - 2)
             fetch(t)
-        compete(PACK - 1)
+        for t in range(SUMMED, PACK):
+            compete(t)
         nc.vector.quantize_mx(out=w3_q[:].bitcast(FP8X4), scales=w3_s[:], in_=w3_bf[:].rearrange("p n j -> p (n j)"))
 
-        chunks = S // CHUNK
-        hid = [sb("hid%d" % c, [P, CHUNK, PACK], BF16) for c in range(chunks)]
-        hid_q = [sb("hid_q%d" % c, [P, CHUNK], U32) for c in range(chunks)]
-        hid_s = [sb("hid_s%d" % c, [P, CHUNK], U8) for c in range(chunks)]
-        res = [sb("res%d" % c, [P, N // P, CHUNK], F32) for c in range(chunks)]
-        r_bank = [psum.tile([P, N // P, CHUNK], F32, name="r_bank%d" % c, tag="bank%d" % c) for c in range(chunks)]
+        chunks = len(CHUNKS)
+        spans = [slice(sum(CHUNKS[:c]), sum(CHUNKS[: c + 1])) for c in range(chunks)]
+        hid = [sb("hid%d" % c, [P, CHUNKS[c], PACK], BF16) for c in range(chunks)]
+        hid_q = [sb("hid_q%d" % c, [P, CHUNKS[c]], U32) for c in range(chunks)]
+        hid_s = [sb("hid_s%d" % c, [P, CHUNKS[c]], U8) for c in range(chunks)]
+        res = [sb("res%d" % c, [P, N // P, CHUNKS[c]], F32) for c in range(chunks)]
+        r_bank = [psum.tile([P, N // P, CHUNKS[c]], F32, name="r_bank%d" % c, tag="bank%d" % c) for c in range(chunks)]
         out_rows = out.rearrange("(a p) s -> p a s", p=P)
 
         def product(c):
-            cols = slice(c * CHUNK, (c + 1) * CHUNK)
+            cols = spans[c]
             nc.vector.tensor_tensor(
                 hid[c][:].rearrange("p (g i) t -> p g t i", i=4),
                 best[:, :, cols].rearrange("p t (g i) -> p g t i", i=4),
@@ -213,7 +223,7 @@ def tile_picked_ysaecr_dif_p_kernel(
                 )
 
         def finish(c):
-            cols = slice(c * CHUNK, (c + 1) * CHUNK)
+            cols = spans[c]
             nc.vector.tensor_tensor(res[c][:], tgt_sb[:, :, cols], r_bank[c][:], ALU.subtract)
             nc.sync.dma_start(out=out_rows[:, :, cols], in_=res[c][:])
 

@@ -20,6 +20,7 @@ PACK = 4
 SUMMED = 2
 CHUNKS = (128, 128, 128, 128)
 WINDOW = 704
+E_ROW = 4
 
 
 def tile_picked_ysaecr_dif_p_kernel(
@@ -46,11 +47,11 @@ def tile_picked_ysaecr_dif_p_kernel(
         thr_sb = sb("thr_sb", [P, PACK], F32)
         unit_sb = sb("unit_sb", [P, PACK], F32)
 
-        def load_scales(queue, plane, scales):
-            for q in range(4):
-                queue.dma_start(
-                    out=plane[32 * q : 32 * q + 4, :].bitcast(I32),
-                    in_=scales[0, 4 * q : 4 * q + 4, :].bitcast(I32),
+        def load_scales(plane, scales, first):
+            for r in range(4):
+                nc.sync.dma_start(
+                    out=plane[first + r : P : 32, :].bitcast(I32),
+                    in_=scales[0, r:16:4, :].bitcast(I32),
                 )
 
         def load_weight(raw, w):
@@ -60,11 +61,11 @@ def tile_picked_ysaecr_dif_p_kernel(
         nc.vector.memset(es[:].bitcast(I32), 0)
         nc.sync.dma_start(offs_sb[:], offs)
         nc.sync.dma_start(out=xw[:].bitcast(I32), in_=x_words[0].rearrange("p n t -> p (n t)").bitcast(I32))
-        load_scales(nc.sync, xs, x_scales)
+        load_scales(xs, x_scales, 0)
         load_weight(w1_raw, w1)
         nc.sync.dma_start(mate_sb[:], mate)
         nc.sync.dma_start(fold_sb[:], fold)
-        load_scales(nc.sync, es, e_scales)
+        load_scales(es, e_scales, E_ROW)
         load_weight(w2_raw, w2)
         nc.sync.dma_start(out=ew[:].bitcast(I32), in_=e_words[0].rearrange("p n t -> p (n t)").bitcast(I32))
         nc.gpsimd.dma_start(out=unit_sb[:], in_=unit.rearrange("(p t) o -> p (t o)", t=PACK))
@@ -72,11 +73,11 @@ def tile_picked_ysaecr_dif_p_kernel(
 
         unit_neg = sb("unit_neg", [P, PACK], F32)
         unit_two = sb("unit_two", [P, PACK], F32)
-        nc.gpsimd.tensor_scalar(unit_neg[:], unit_sb[:], -1.0, 0.0, ALU.mult, ALU.add)
-        nc.gpsimd.tensor_scalar(unit_two[:], unit_sb[:], 2.0, 0.0, ALU.mult, ALU.add)
+        nc.scalar.activation(unit_neg[:], unit_sb[:], ACT.Copy, scale=-1.0)
+        nc.scalar.activation(unit_two[:], unit_sb[:], ACT.Copy, scale=2.0)
 
         thr_part = sb("thr_part", [P, PACK], F32)
-        nc.gpsimd.tensor_scalar(thr_part[:], thr_sb[:], 0.8, 0.0, ALU.mult, ALU.add)
+        nc.scalar.activation(thr_part[:], thr_sb[:], ACT.Copy, scale=0.8)
 
         xw_g = sb("xw_g", [P, S], U32)
         xs_g = sb("xs_g", [P, S], U8)
@@ -108,7 +109,7 @@ def tile_picked_ysaecr_dif_p_kernel(
         nc.sync.dma_start(out=w3_raw[:], in_=w3.rearrange("(p j) n -> p j n", j=PACK))
         quantize(w1_q, w1_s, w1_bf, 1)
         quantize(w1_q, w1_s, w1_bf, 0)
-        es_g = sb("es_g", [P, S], U8, tag="w1_bf")
+        es_g = sb("es_g", [P, S], U8)
         nc.vector.tensor_copy(out=es_g[:], in_=es[:].indirect(mate_sb[:]))
         deal(nc.scalar.copy, w2_bf, w2_raw, 0)
         deal(nc.vector.tensor_copy, w2_bf, w2_raw, 1)
@@ -121,19 +122,19 @@ def tile_picked_ysaecr_dif_p_kernel(
             cols = slice(t * P, (t + 1) * P)
             nc.tensor.matmul_mx(
                 out=bank[:], lhsT=wq[:, cols].bitcast(FP8X4), lhsT_scale=ws[:, cols],
-                rhs=words[:].bitcast(FP8X4), rhs_scale=scales[:], start=start, stop=stop,
+                rhs=words[:].bitcast(FP8X4), rhs_scale=scales, start=start, stop=stop,
             )
 
         y_bank = [psum.tile([P, S], F32, name="y_bank%d" % t, tag="bank%d" % t) for t in range(PACK)]
         e_bank = [psum.tile([P, S], F32, name="e_bank%d" % t, tag="bank%d" % (PACK + t)) for t in range(PACK)]
         lat = [sb("lat%d" % t, [P, WINDOW], F32) for t in range(PACK)]
         for t in range(PACK):
-            nc.gpsimd.memset(lat[t][:, S:], 0.0)
+            nc.vector.memset(lat[t][:, S:], 0.0)
         y_sb = sb("y_sb", [P, PACK - 1, S], F32, tag="w2_raw")
         for t in reversed(range(PACK)):
-            encode(y_bank[t], w1_q, w1_s, xw_g, xs_g, t, True, True)
+            encode(y_bank[t], w1_q, w1_s, xw_g, xs_g[:], t, True, True)
         for t in range(SUMMED):
-            encode(e_bank[t], w1_q, w1_s, xw_g, xs_g, t, True, False)
+            encode(e_bank[t], w1_q, w1_s, xw_g, xs_g[:], t, True, False)
         for t in range(SUMMED, PACK):
             nc.scalar.copy(out=y_sb[:, t - SUMMED, :], in_=y_bank[t][:])
         nc.scalar.activation(y_sb[:, 2, :], y_bank[1][:], ACT.Copy, scale=unit_two[:, 1:2])
@@ -144,7 +145,7 @@ def tile_picked_ysaecr_dif_p_kernel(
         nc.vector.tensor_scalar(y_first[:], y_bank[0][:], unit_two[:, 0:1], None, ALU.mult)
         twice = [y_first[:], y_sb[:, 2, :]]
         for t in (0, 2, 1, 3):
-            encode(e_bank[t], w2_q, w2_s, ew_g, es_g, t, t >= SUMMED, True)
+            encode(e_bank[t], w2_q, w2_s, ew_g, es_g[E_ROW:P, :], t, t >= SUMMED, True)
 
         diff = sb("diff", [P, PACK, S], F32)
         best = sb("best", [P, PACK, S], F32)

from contextlib import ExitStack

import concourse.mybir as mybir

K, T, S, N, H, W = 512, 1024, 512, 256, 512, 2048
FLOPS = 2 * (2 * K * H * S + H * N * S)

F32 = mybir.dt.float32
BF16 = mybir.dt.bfloat16
I32 = mybir.dt.int32
U32 = mybir.dt.uint32
U16 = mybir.dt.uint16
U8 = mybir.dt.uint8
FP8X4 = mybir.dt.float8_e4m3fn_x4
ALU = mybir.AluOpType
ACT = mybir.ActivationFunctionType

P = 128
PACK = 4
SUMMED = 2
CHUNKS = (128, 128, 128, 128)
WINDOW = 704
E_ROW = 4


def tile_picked_ysaecr_dif_p_kernel(
    tc, x_words, x_scales, w1, e_words, e_scales, w2, thr, unit, w3, tgt, offs, mate, fold, out
):
    nc = tc.nc
    with ExitStack() as ctx:
        keep = ctx.enter_context(tc.tile_pool(name="keep", bufs=1))
        psum = ctx.enter_context(tc.psum_pool(name="psum", bufs=1))

        def sb(name, shape, dtype, tag=None):
            return keep.tile(shape, dtype, name=name, tag=tag or name, align_bytes=64)

        offs_sb = sb("offs_sb", [P, S // 16], U16)
        mate_sb = sb("mate_sb", [P, S // 16], U16)
        fold_sb = sb("fold_sb", [P, S // 16], U16)
        xw = sb("xw", [P, T], U32)
        xs = sb("xs", [P, T], U8)
        ew = sb("ew", [P, W], U32)
        es = sb("es", [P, W], U8)
        half = H // 2
        w1_raw = sb("w1_raw", [P, PACK, H], F32)
        w2_raw = sb("w2_raw", [P, PACK, H], F32)
        thr_sb = sb("thr_sb", [P, PACK], F32)
        unit_sb = sb("unit_sb", [P, PACK], F32)

        def load_scales(plane, scales, first):
            for r in range(4):
                nc.sync.dma_start(
                    out=plane[first + r : P : 32, :].bitcast(I32),
                    in_=scales[0, r:16:4, :].bitcast(I32),
                )

        def load_weight(raw, w):
            nc.sync.dma_start(out=raw[:], in_=w.rearrange("(p j) c -> p j c", j=PACK))

        nc.vector.memset(xs[:].bitcast(I32), 0)
        nc.vector.memset(es[:].bitcast(I32), 0)
        nc.sync.dma_start(offs_sb[:], offs)
        nc.sync.dma_start(out=xw[:].bitcast(I32), in_=x_words[0].rearrange("p n t -> p (n t)").bitcast(I32))
        load_scales(xs, x_scales, 0)
        load_weight(w1_raw, w1)
        nc.sync.dma_start(mate_sb[:], mate)
        nc.sync.dma_start(fold_sb[:], fold)
        load_scales(es, e_scales, E_ROW)
        load_weight(w2_raw, w2)
        nc.sync.dma_start(out=ew[:].bitcast(I32), in_=e_words[0].rearrange("p n t -> p (n t)").bitcast(I32))
        nc.gpsimd.dma_start(out=unit_sb[:], in_=unit.rearrange("(p t) o -> p (t o)", t=PACK))
        nc.gpsimd.dma_start(out=thr_sb[:], in_=thr.rearrange("(p t) o -> p (t o)", t=PACK))

        unit_neg = sb("unit_neg", [P, PACK], F32)
        unit_two = sb("unit_two", [P, PACK], F32)
        nc.scalar.activation(unit_neg[:], unit_sb[:], ACT.Copy, scale=-1.0)
        nc.scalar.activation(unit_two[:], unit_sb[:], ACT.Copy, scale=2.0)

        thr_part = sb("thr_part", [P, PACK], F32)
        nc.scalar.activation(thr_part[:], thr_sb[:], ACT.Copy, scale=0.8)

        xw_g = sb("xw_g", [P, S], U32)
        xs_g = sb("xs_g", [P, S], U8)

        def deal(copy, grouped, raw, h):
            pair = slice(2 * h, 2 * h + 2)
            dst = grouped[:, pair, :, :].rearrange("p t m j -> p m j t")
            copy(out=dst, in_=raw[:].rearrange("p j (m t) -> p m j t", t=PACK)[:, :, :, pair])

        def quantize(codes, scales, grouped, h):
            cols = slice(h * half, (h + 1) * half)
            nc.vector.quantize_mx(
                out=codes[:, cols].bitcast(FP8X4), scales=scales[:, cols],
                in_=grouped[:, 2 * h : 2 * h + 2, :, :].rearrange("p t m j -> p (t m j)"),
            )

        w1_bf = sb("w1_bf", [P, PACK, P, PACK], BF16)
        w2_bf = sb("w2_bf", [P, PACK, P, PACK], BF16)
        w1_q = sb("w1_q", [P, H], U32)
        w1_s = sb("w1_s", [P, H], U8)
        w2_q = sb("w2_q", [P, H], U32)
        w2_s = sb("w2_s", [P, H], U8)

        nc.vector.tensor_copy(out=xw_g[:], in_=xw[:].indirect(offs_sb[:]))
        nc.vector.tensor_copy(out=xs_g[:], in_=xs[:].indirect(offs_sb[:]))
        deal(nc.scalar.copy, w1_bf, w1_raw, 0)
        deal(nc.vector.tensor_copy, w1_bf, w1_raw, 1)
        w3_raw = sb("w3_raw", [P, PACK, N], F32, tag="w1_raw")
        nc.sync.dma_start(out=w3_raw[:], in_=w3.rearrange("(p j) n -> p j n", j=PACK))
        quantize(w1_q, w1_s, w1_bf, 1)
        quantize(w1_q, w1_s, w1_bf, 0)
        es_g = sb("es_g", [P, S], U8)
        nc.vector.tensor_copy(out=es_g[:], in_=es[:].indirect(mate_sb[:]))
        deal(nc.scalar.copy, w2_bf, w2_raw, 0)
        deal(nc.vector.tensor_copy, w2_bf, w2_raw, 1)
        tgt_sb = sb("tgt_sb", [P, N // P, S], F32, tag="xw")
        nc.sync.dma_start(out=tgt_sb[:], in_=tgt.rearrange("(a p) s -> p a s", p=P))
        quantize(w2_q, w2_s, w2_bf, 1)
        quantize(w2_q, w2_s, w2_bf, 0)

        def encode(bank, wq, ws, words, scales, t, start, stop):
            cols = slice(t * P, (t + 1) * P)
            nc.tensor.matmul_mx(
                out=bank[:], lhsT=wq[:, cols].bitcast(FP8X4), lhsT_scale=ws[:, cols],
                rhs=words[:].bitcast(FP8X4), rhs_scale=scales, start=start, stop=stop,
            )

        y_bank = [psum.tile([P, S], F32, name="y_bank%d" % t, tag="bank%d" % t) for t in range(PACK)]
        e_bank = [psum.tile([P, S], F32, name="e_bank%d" % t, tag="bank%d" % (PACK + t)) for t in range(PACK)]
        lat = [sb("lat%d" % t, [P, WINDOW], F32) for t in range(PACK)]
        for t in range(PACK):
            nc.vector.memset(lat[t][:, S:], 0.0)
        y_sb = sb("y_sb", [P, PACK - 1, S], F32, tag="w2_raw")
        for t in reversed(range(PACK)):
            encode(y_bank[t], w1_q, w1_s, xw_g, xs_g[:], t, True, True)
        for t in range(SUMMED):
            encode(e_bank[t], w1_q, w1_s, xw_g, xs_g[:], t, True, False)
        for t in range(SUMMED, PACK):
            nc.scalar.copy(out=y_sb[:, t - SUMMED, :], in_=y_bank[t][:])
        nc.scalar.activation(y_sb[:, 2, :], y_bank[1][:], ACT.Copy, scale=unit_two[:, 1:2])

        ew_g = sb("ew_g", [P, S], U32, tag="es")
        nc.vector.tensor_copy(out=ew_g[:], in_=ew[:].indirect(mate_sb[:]))
        y_first = sb("y_first", [P, S], F32, tag="ew")
        nc.vector.tensor_scalar(y_first[:], y_bank[0][:], unit_two[:, 0:1], None, ALU.mult)
        twice = [y_first[:], y_sb[:, 2, :]]
        for t in (0, 2, 1, 3):
            encode(e_bank[t], w2_q, w2_s, ew_g, es_g[E_ROW:P, :], t, t >= SUMMED, True)

        diff = sb("diff", [P, PACK, S], F32)
        best = sb("best", [P, PACK, S], F32)
        ff = [sb("ff%d" % t, [P, S], F32) for t in range(PACK)]
        ye_sb = {t: sb("ye_sb%d" % t, [P, S], F32) for t in range(SUMMED, PACK)}
        total = {t: sb("total%d" % t, [P, S], F32) for t in range(SUMMED, PACK)}
        plain = {t: sb("plain%d" % t, [P, S], F32) for t in range(SUMMED, PACK)}
        for t in range(SUMMED):
            total[t] = e_bank[t]

        def latent(t):
            nc.scalar.activation(lat[t][:, :S], total[t][:], ACT.Relu, bias=thr_part[:, t : t + 1], scale=0.8)

        def scaled_diff(t):
            nc.vector.scalar_tensor_tensor(diff[:, t, :], e_bank[t][:], unit_neg[:, t : t + 1], twice[t], ALU.mult, ALU.add)

        def fetch(t):
            nc.vector.tensor_copy(out=ff[t][:], in_=lat[t][:].indirect(fold_sb[:]))

        def compete(t):
            nc.vector.scalar_tensor_tensor(best[:, t, :], total[t][:], thr_sb[:, t : t + 1], ff[t][:], ALU.add, ALU.max)

        for t in range(SUMMED):
            latent(t)
            nc.scalar.copy(out=ye_sb[SUMMED + t][:], in_=e_bank[SUMMED + t][:])
        for t in range(SUMMED, PACK):
            nc.gpsimd.tensor_tensor(total[t][:], y_sb[:, t - SUMMED, :], ye_sb[t][:], ALU.add)
        latent(2)
        scaled_diff(0)
        fetch(0)
        scaled_diff(1)
        fetch(1)
        w3_bf = sb("w3_bf", [P, N, PACK], BF16, tag="lat1")
        w3_q = sb("w3_q", [P, N], U32)
        w3_s = sb("w3_s", [P, N], U8)
        nc.scalar.copy(
            out=w3_bf[:].rearrange("p (c i) j -> p c j i", i=4),
            in_=w3_raw[:].rearrange("p j (c i) -> p c j i", i=4),
        )
        latent(3)
        for t in range(SUMMED, PACK):
            nc.gpsimd.tensor_tensor(plain[t][:], y_sb[:, t - SUMMED, :], ye_sb[t][:], ALU.subtract)
            nc.scalar.activation(diff[:, t, :], plain[t][:], ACT.Copy, scale=unit_sb[:, t : t + 1])
        for t in range(SUMMED, PACK):
            compete(t - 2)
            fetch(t)
        for t in range(SUMMED, PACK):
            compete(t)
        nc.vector.quantize_mx(out=w3_q[:].bitcast(FP8X4), scales=w3_s[:], in_=w3_bf[:].rearrange("p n j -> p (n j)"))

        chunks = len(CHUNKS)
        spans = [slice(sum(CHUNKS[:c]), sum(CHUNKS[: c + 1])) for c in range(chunks)]
        hid = [sb("hid%d" % c, [P, CHUNKS[c], PACK], BF16) for c in range(chunks)]
        hid_q = [sb("hid_q%d" % c, [P, CHUNKS[c]], U32) for c in range(chunks)]
        hid_s = [sb("hid_s%d" % c, [P, CHUNKS[c]], U8) for c in range(chunks)]
        res = [sb("res%d" % c, [P, N // P, CHUNKS[c]], F32) for c in range(chunks)]
        r_bank = [psum.tile([P, N // P, CHUNKS[c]], F32, name="r_bank%d" % c, tag="bank%d" % c) for c in range(chunks)]
        out_rows = out.rearrange("(a p) s -> p a s", p=P)

        def product(c):
            cols = spans[c]
            nc.vector.tensor_tensor(
                hid[c][:].rearrange("p (g i) t -> p g t i", i=4),
                best[:, :, cols].rearrange("p t (g i) -> p g t i", i=4),
                diff[:, :, cols].rearrange("p t (g i) -> p g t i", i=4),
                ALU.mult,
            )

        def decode(c):
            nc.vector.quantize_mx(out=hid_q[c][:].bitcast(FP8X4), scales=hid_s[c][:], in_=hid[c][:].rearrange("p s t -> p (s t)"))
            for a in range(N // P):
                rows = slice(a * P, (a + 1) * P)
                nc.tensor.matmul_mx(
                    out=r_bank[c][:, a, :], lhsT=w3_q[:, rows].bitcast(FP8X4), lhsT_scale=w3_s[:, rows],
                    rhs=hid_q[c][:].bitcast(FP8X4), rhs_scale=hid_s[c][:], start=True, stop=True,
                )

        def finish(c):
            cols = spans[c]
            nc.vector.tensor_tensor(res[c][:], tgt_sb[:, :, cols], r_bank[c][:], ALU.subtract)
            nc.sync.dma_start(out=out_rows[:, :, cols], in_=res[c][:])

        for step in range(chunks + 2):
            if step < chunks:
                product(step)
            if 1 <= step <= chunks:
                decode(step - 1)
            if step >= 2:
                finish(step - 2)
